import numpy as np
import ml_dtypes


def mxq(x, axis, fmt="e4m3"):
    dtype, down = {"e4m3": (ml_dtypes.float8_e4m3fn, 7), "e5m2": (ml_dtypes.float8_e5m2, 14)}[fmt]
    v = np.moveaxis(np.asarray(x, np.float32).astype(ml_dtypes.bfloat16).astype(np.float64), axis, -1)
    blocks = v.reshape(v.shape[:-1] + (-1, 32))
    amax = np.abs(blocks).max(-1, keepdims=True)
    byte = np.maximum(np.where(amax > 0, np.frexp(amax)[1] - 1 + 127, 0) - down, 1)
    scale = np.exp2(byte - 127.0)
    codes = (blocks / scale).astype(np.float32).astype(dtype).astype(np.float64)
    return np.moveaxis((codes * scale).reshape(v.shape), -1, axis)


WIDE = False


def mx_kscale(k):
    if not WIDE:
        return np.ones(k)
    levels = np.array([30, -30])
    if k % 512:
        return np.exp2(np.random.permutation(np.resize(levels, k // 32))).repeat(32)
    a = np.empty((k // 512, 16))
    for p in range(k // 512):
        a[p, :8] = np.random.permutation(np.resize(levels, 8))
        for g in range(8):
            far = levels[np.abs(levels - a[p, g]) >= 10]
            a[p, g + 8] = far[np.random.randint(len(far))]
    return np.exp2(a.ravel()).repeat(32)


def f64(x):
    return np.asarray(x).astype(np.float64)


def striped(idx):
    return np.tile(np.asarray(idx).reshape(-1, 16).T, (8, 1)).astype(np.uint16)


def unstriped(offs):
    return offs[:16].T.reshape(-1).astype(np.int64)


E2M1 = np.array([0.0, 0.5, 1.0, 1.5, 2.0, 3.0, 4.0, 6.0, -0.0, -0.5, -1.0, -1.5, -2.0, -3.0, -4.0, -6.0])


def pack_weight(w, fmt):
    k, n = w.shape
    w = f64(np.asarray(w, np.float32).astype(ml_dtypes.bfloat16)).reshape(k // 32, 32, n)
    amax = np.abs(w).max(1)
    if fmt in ("e4m3", "e5m2"):
        byte = np.frexp(amax)[1] - 1 + 127 - (7 if fmt == "e4m3" else 14)
    else:
        mant, ex = np.frexp(amax / 6.0)
        byte = np.where(mant > 0.5, ex, ex - 1) + 127
    byte = np.clip(np.where(amax > 0, byte, 1), 1, 254)
    scaled = (w * np.exp2(127.0 - byte)[:, None, :]).reshape(k, n).astype(np.float32)
    by_word = np.ascontiguousarray(scaled.reshape(k // 512, 128, 4, n).transpose(0, 1, 3, 2))
    if fmt in ("e4m3", "e5m2"):
        words = by_word.astype(ml_dtypes.float8_e4m3fn if fmt == "e4m3" else ml_dtypes.float8_e5m2).view(np.uint8)
    else:
        c = by_word.astype(ml_dtypes.float4_e2m1fn).view(np.uint8) & 0xF
        words = (c[..., 0::2] | (c[..., 1::2] << 4)).reshape(k // 512, 128, 2 * n)
    return np.ascontiguousarray(words), np.ascontiguousarray(byte.astype(np.uint8).reshape(k // 512, 16, n))


def unpack_weight(words, scales, fmt):
    g, _, n = scales.shape
    words = np.ascontiguousarray(words).reshape(g, 128, n, -1)
    if fmt in ("e4m3", "e5m2"):
        vals = words.view(ml_dtypes.float8_e4m3fn if fmt == "e4m3" else ml_dtypes.float8_e5m2).astype(np.float64)
    else:
        nib = np.empty((g, 128, n, 4), np.uint8)
        nib[..., 0::2] = words & 0xF
        nib[..., 1::2] = words >> 4
        vals = E2M1[nib]
    vals = vals * np.repeat(np.exp2(scales.astype(np.float64) - 127.0), 8, axis=1)[..., None]
    return vals.transpose(0, 1, 3, 2).reshape(g * 512, n)


K, F, T, Z, J, R, C, O, N = 512, 512, 1024, 1024, 256, 512, 512, 128, 256


def setup_inputs():
    n = np.random.standard_normal
    idx = np.random.permutation(T)[:J]
    idx2 = np.random.permutation(Z)[:J]
    idx3 = np.random.permutation(C)[:J]
    idx4 = np.random.permutation(C)[:O]
    idx5 = np.random.permutation(C)[:O]
    idx6 = np.random.permutation(T)[:O]
    fk = mx_kscale(K)
    fr = mx_kscale(R)
    ff = mx_kscale(F)
    xtp = pack_weight(n((K, T)) / fk[:, None], "e2m1")
    wp = pack_weight(n((K, R)) * 1 / np.sqrt(K) * fk[:, None] * fr, "e5m2")
    xop = pack_weight(n((F, Z)) / ff[:, None], "e5m2")
    w0p = pack_weight(n((F, R)) * 1 / np.sqrt(F) * ff[:, None] * fr, "e4m3")
    wbp = pack_weight(n((R, N)) * 1 / np.sqrt(R) / fr[:, None], "e4m3")
    wsp = pack_weight(n((K, N)) * 1 / np.sqrt(K) * fk[:, None], "e4m3")
    return {
        "xt_words": xtp[0],
        "xt_scales": xtp[1],
        "w_words": wp[0],
        "w_scales": wp[1],
        "xo_words": xop[0],
        "xo_scales": xop[1],
        "w0_words": w0p[0],
        "w0_scales": w0p[1],
        "wb_words": wbp[0],
        "wb_scales": wbp[1],
        "ws_words": wsp[0],
        "ws_scales": wsp[1],
        "offs": striped(idx),
        "offs2": striped(idx2),
        "offs3": striped(idx3),
        "offs4": striped(idx4),
        "offs5": striped(idx5),
        "offs6": striped(idx6),
    }


def reference(xt_words, xt_scales, w_words, w_scales, xo_words, xo_scales, w0_words, w0_scales, wb_words, wb_scales, ws_words, ws_scales, offs, offs2, offs3, offs4, offs5, offs6):
    idx = unstriped(offs)
    idx2 = unstriped(offs2)
    idx3 = unstriped(offs3)
    idx4 = unstriped(offs4)
    idx5 = unstriped(offs5)
    idx6 = unstriped(offs6)
    xtu = unpack_weight(xt_words, xt_scales, "e2m1")
    wu = unpack_weight(w_words, w_scales, "e5m2")
    xou = unpack_weight(xo_words, xo_scales, "e5m2")
    w0u = unpack_weight(w0_words, w0_scales, "e4m3")
    wbu = unpack_weight(wb_words, wb_scales, "e4m3")
    wsu = unpack_weight(ws_words, ws_scales, "e4m3")
    xtidxg = xtu[:, idx]
    xoidx2g = xou[:, idx2]
    a = wu.T @ xtidxg + w0u.T @ xoidx2g
    pw = np.zeros((R, C))
    pw[:, idx3] = a
    hid = np.maximum(pw[:, idx4], pw[:, idx5])
    hidq = mxq(hid, 0, "e5m2")
    xtidx6g = xtu[:, idx6]
    y = wbu.T @ hidq + wsu.T @ xtidx6g
    return y

@@ -1,0 +1,181 @@
+from contextlib import ExitStack
+
+import concourse.mybir as mybir
+
+F32 = mybir.dt.float32
+BF16 = mybir.dt.bfloat16
+I32 = mybir.dt.int32
+U32 = mybir.dt.uint32
+U16 = mybir.dt.uint16
+U8 = mybir.dt.uint8
+E4M3 = mybir.dt.float8_e4m3fn_x4
+E5M2 = mybir.dt.float8_e5m2_x4
+E2M1 = mybir.dt.float4_e2m1fn_x4
+COPY = mybir.ActivationFunctionType.Copy
+MAX = mybir.AluOpType.max
+
+P = 128
+PACK = 4
+T, Z, J, R, C, O, N = 1024, 1024, 256, 512, 512, 128, 256
+FLOPS = 2 * 512 * (2 * R * J + 2 * N * O)
+
+
+def tile_list_readtwice_bank_further_plain_kernel(
+    tc, xt_words, xt_scales, w_words, w_scales, xo_words, xo_scales, w0_words, w0_scales,
+    wb_words, wb_scales, ws_words, ws_scales, offs, offs2, offs3, offs4, offs5, offs6, out,
+):
+    nc = tc.nc
+    with ExitStack() as ctx:
+        sb = ctx.enter_context(tc.tile_pool(name="sb", bufs=1))
+        ps = ctx.enter_context(tc.psum_pool(name="ps", bufs=1))
+
+        def load_list(src, name):
+            tile = sb.tile(list(src.shape), U16, name=name)
+            nc.sync.dma_start(tile[:], src)
+            return tile
+
+        def load_words(src, width, dtype, name):
+            tile = sb.tile([P, width], dtype, name=name, align_bytes=64)
+            nc.sync.dma_start(tile[:].bitcast(I32), src.bitcast(I32))
+            return tile
+
+        def load_plane(src, clear, queue, name):
+            tile = sb.tile([P, src.shape[2]], U8, name=name, align_bytes=64)
+            clear.memset(tile[:].bitcast(I32), 0)
+            for q in range(4):
+                queue.dma_start(tile[32 * q : 32 * q + 4, :].bitcast(I32), src[0, 4 * q : 4 * q + 4, :].bitcast(I32))
+            return tile
+
+        def bytes_of(words):
+            return words[0].rearrange("p n t -> p (n t)")
+
+        def gather(window, offsets, dtype, name):
+            tile = sb.tile([P, 16 * offsets.shape[1]], dtype, name=name, align_bytes=64)
+            nc.vector.tensor_copy(tile[:], window[:].indirect(offsets[:]))
+            return tile
+
+        def deal_words(words, name):
+            dealt = sb.tile([P, R], U32, name=name, align_bytes=64)
+            nc.scalar.copy(
+                dealt[:].rearrange("p (t c i) -> p c t i", t=PACK, i=4),
+                words[:].rearrange("p (c i t) -> p c t i", t=PACK, i=4),
+            )
+            return dealt
+
+        def deal_plane(plane, name):
+            dealt = sb.tile([P, R], U8, name=name, align_bytes=64)
+            nc.vector.tensor_copy(
+                dealt[:].rearrange("p (t m) -> p t m", t=PACK),
+                plane[:].rearrange("p (m t) -> p t m", t=PACK),
+            )
+            return dealt
+
+        idx = load_list(offs, "idx")
+        xt_w = load_words(xt_words[0], T, U16, "xt_w")
+        idx2 = load_list(offs2, "idx2")
+        xo_w = load_words(bytes_of(xo_words), Z, U32, "xo_w")
+        xt_s = load_plane(xt_scales, nc.vector, nc.scalar, "xt_s")
+        xo_s = load_plane(xo_scales, nc.gpsimd, nc.sync, "xo_s")
+        w0_s = load_plane(w0_scales, nc.gpsimd, nc.gpsimd, "w0_s")
+        w_w = load_words(bytes_of(w_words), R, U32, "w_w")
+        w0_w = load_words(bytes_of(w0_words), R, U32, "w0_w")
+        w_s = load_plane(w_scales, nc.vector, nc.sync, "w_s")
+        idx6 = load_list(offs6, "idx6")
+        idx3 = load_list(offs3, "idx3")
+        idx4 = load_list(offs4, "idx4")
+        idx5 = load_list(offs5, "idx5")
+        ws_w = load_words(bytes_of(ws_words), N, U32, "ws_w")
+        wb_w = load_words(bytes_of(wb_words), N, U32, "wb_w")
+        ws_s = load_plane(ws_scales, nc.vector, nc.sync, "ws_s")
+        wb_s = load_plane(wb_scales, nc.vector, nc.sync, "wb_s")
+
+        boards = [sb.tile([P, C], F32, name="board%d" % t) for t in range(PACK)]
+        for board in boards:
+            nc.vector.memset(board[:], 0.0)
+
+        tok_w = gather(xt_w, idx, U16, "tok_w")
+        note_w = gather(xo_w, idx2, U32, "note_w")
+        tok_s = gather(xt_s, idx, U8, "tok_s")
+        note_s = gather(xo_s, idx2, U8, "note_s")
+        wd_w = deal_words(w_w, "wd_w")
+        w0d_w = deal_words(w0_w, "w0d_w")
+        wd_s = deal_plane(w_s, "wd_s")
+        w0d_s = deal_plane(w0_s, "w0d_s")
+
+        banks = [ps.tile([P, J], F32, name="a_bank%d" % t) for t in range(PACK)]
+        for t in range(PACK):
+            cols = slice(P * t, P * (t + 1))
+            nc.tensor.matmul_mx(
+                out=banks[t][:], lhsT=wd_w[:, cols].bitcast(E5M2), lhsT_scale=wd_s[:, cols],
+                rhs=tok_w[:].bitcast(E2M1), rhs_scale=tok_s[:], start=True, stop=False,
+            )
+            nc.tensor.matmul_mx(
+                out=banks[t][:], lhsT=w0d_w[:, cols].bitcast(E4M3), lhsT_scale=w0d_s[:, cols],
+                rhs=note_w[:].bitcast(E5M2), rhs_scale=note_s[:], start=False, stop=True,
+            )
+
+        far_w = gather(xt_w, idx6, U16, "far_w")
+        far_s = gather(xt_s, idx6, U8, "far_s")
+        y_banks = [ps.tile([P, O], F32, name="y_bank%d" % u) for u in range(N // P)]
+        for u in range(N // P):
+            cols = slice(P * u, P * (u + 1))
+            nc.tensor.matmul_mx(
+                out=y_banks[u][:], lhsT=ws_w[:, cols].bitcast(E4M3), lhsT_scale=ws_s[:, cols],
+                rhs=far_w[:].bitcast(E2M1), rhs_scale=far_s[:], start=True, stop=False,
+            )
+
+        first = sb.tile([P, PACK, O], F32, name="first")
+        second = sb.tile([P, PACK, O], F32, name="second")
+        hid = sb.tile([P, O * PACK], BF16, name="hid", align_bytes=64)
+        hid_view = hid[:].rearrange("p (c i t) -> p c t i", t=PACK, i=4)
+        a = [sb.tile([P, J], F32, name="a%d" % t) for t in range(PACK)]
+
+        def look_v(dst, t, offsets):
+            nc.vector.tensor_copy(dst[:, t, :], boards[t][:].indirect(offsets[:]))
+
+        def look_s(dst, t, offsets):
+            nc.scalar.activation(dst[:, t, :], boards[t][:].indirect(offsets[:]), COPY)
+
+        def larger(rows):
+            nc.vector.tensor_tensor(
+                hid_view[:, :, rows, :],
+                first[:, rows, :].rearrange("p t (c i) -> p c t i", i=4),
+                second[:, rows, :].rearrange("p t (c i) -> p c t i", i=4),
+                MAX,
+            )
+
+        nc.vector.tensor_copy(a[0][:], banks[0][:])
+        nc.scalar.copy(a[1][:], banks[1][:])
+        nc.scalar.copy(a[2][:], banks[2][:])
+        nc.vector.tensor_copy(boards[0][:].indirect(idx3[:]), a[0][:])
+        nc.scalar.activation(boards[1][:].indirect(idx3[:]), a[1][:], COPY)
+        nc.vector.tensor_copy(boards[2][:].indirect(idx3[:]), a[2][:])
+        nc.scalar.copy(a[3][:], banks[3][:])
+        look_s(second, 1, idx5)
+        nc.scalar.activation(boards[3][:].indirect(idx3[:]), a[3][:], COPY)
+        look_v(first, 0, idx4)
+        look_v(second, 0, idx5)
+        look_v(first, 1, idx4)
+        look_v(first, 2, idx4)
+        larger(slice(0, 2))
+        look_v(second, 2, idx5)
+        look_s(first, 3, idx4)
+        look_s(second, 3, idx5)
+        larger(slice(2, 4))
+
+        hid_w = sb.tile([P, O], U32, name="hid_w", align_bytes=64)
+        hid_s = sb.tile([P, O], U8, name="hid_s", align_bytes=64)
+        nc.vector.quantize_mx(out=hid_w[:].bitcast(E5M2), scales=hid_s[:], in_=hid[:])
+
+        for u in range(N // P):
+            cols = slice(P * u, P * (u + 1))
+            nc.tensor.matmul_mx(
+                out=y_banks[u][:], lhsT=wb_w[:, cols].bitcast(E4M3), lhsT_scale=wb_s[:, cols],
+                rhs=hid_w[:].bitcast(E5M2), rhs_scale=hid_s[:], start=False, stop=True,
+            )
+        y0 = sb.tile([P, O], F32, name="y0")
+        nc.vector.tensor_copy(y0[:], y_banks[0][:])
+        nc.sync.dma_start(out[0:P, :], y0[:])
+        y1 = sb.tile([P, O], F32, name="y1")
+        nc.scalar.copy(y1[:], y_banks[1][:])
+        nc.scalar.dma_start(out[P : 2 * P, :], y1[:])

@@ -39,12 +39,14 @@ def tile_list_readtwice_bank_further_plain_kernel(
             nc.sync.dma_start(tile[:].bitcast(I32), src.bitcast(I32))
             return tile
 
-        def load_plane(src, clear, queue, name):
+        def plane_for(src, clear, name):
             tile = sb.tile([P, src.shape[2]], U8, name=name, align_bytes=64)
             clear.memset(tile[:].bitcast(I32), 0)
-            for q in range(4):
-                queue.dma_start(tile[32 * q : 32 * q + 4, :].bitcast(I32), src[0, 4 * q : 4 * q + 4, :].bitcast(I32))
             return tile
+
+        def load_rows(tile, src, quadrants):
+            for q in quadrants:
+                nc.sync.dma_start(tile[32 * q : 32 * q + 4, :].bitcast(I32), src[0, 4 * q : 4 * q + 4, :].bitcast(I32))
 
         def bytes_of(words):
             return words[0].rearrange("p n t -> p (n t)")
@@ -54,53 +56,65 @@ def tile_list_readtwice_bank_further_plain_kernel(
             nc.vector.tensor_copy(tile[:], window[:].indirect(offsets[:]))
             return tile
 
-        def deal_words(words, name):
+        def deal_words(words, parts, name):
             dealt = sb.tile([P, R], U32, name=name, align_bytes=64)
-            nc.scalar.copy(
-                dealt[:].rearrange("p (t c i) -> p c t i", t=PACK, i=4),
-                words[:].rearrange("p (c i t) -> p c t i", t=PACK, i=4),
-            )
+            for t0 in range(0, PACK, PACK // parts):
+                ts = slice(t0, t0 + PACK // parts)
+                nc.scalar.copy(
+                    dealt[:].rearrange("p (t c i) -> p c t i", t=PACK, i=4)[:, :, ts, :],
+                    words[:].rearrange("p (c i t) -> p c t i", t=PACK, i=4)[:, :, ts, :],
+                )
             return dealt
 
-        def deal_plane(plane, name):
+        def deal_plane(plane, parts, name):
             dealt = sb.tile([P, R], U8, name=name, align_bytes=64)
-            nc.vector.tensor_copy(
-                dealt[:].rearrange("p (t m) -> p t m", t=PACK),
-                plane[:].rearrange("p (m t) -> p t m", t=PACK),
-            )
+            for t0 in range(0, PACK, PACK // parts):
+                ts = slice(t0, t0 + PACK // parts)
+                nc.vector.tensor_copy(
+                    dealt[:].rearrange("p (t m) -> p t m", t=PACK)[:, ts, :],
+                    plane[:].rearrange("p (m t) -> p t m", t=PACK)[:, ts, :],
+                )
             return dealt
+
+        xt_s = plane_for(xt_scales, nc.vector, "xt_s")
+        xo_s = plane_for(xo_scales, nc.vector, "xo_s")
+        w_s = plane_for(w_scales, nc.vector, "w_s")
+        w0_s = plane_for(w0_scales, nc.vector, "w0_s")
+        ws_s = plane_for(ws_scales, nc.vector, "ws_s")
+        wb_s = plane_for(wb_scales, nc.vector, "wb_s")
 
         idx = load_list(offs, "idx")
-        xt_w = load_words(xt_words[0], T, U16, "xt_w")
         idx2 = load_list(offs2, "idx2")
+        xt_w = load_words(xt_words[0], T, U16, "xt_w")
+        load_rows(xt_s, xt_scales, range(4))
         xo_w = load_words(bytes_of(xo_words), Z, U32, "xo_w")
-        xt_s = load_plane(xt_scales, nc.vector, nc.scalar, "xt_s")
-        xo_s = load_plane(xo_scales, nc.gpsimd, nc.sync, "xo_s")
-        w0_s = load_plane(w0_scales, nc.gpsimd, nc.gpsimd, "w0_s")
+        load_rows(xo_s, xo_scales, range(4))
+        load_rows(w_s, w_scales, range(2))
         w_w = load_words(bytes_of(w_words), R, U32, "w_w")
         w0_w = load_words(bytes_of(w0_words), R, U32, "w0_w")
-        w_s = load_plane(w_scales, nc.vector, nc.sync, "w_s")
+        load_rows(w_s, w_scales, range(2, 4))
+        load_rows(w0_s, w0_scales, range(4))
         idx6 = load_list(offs6, "idx6")
         idx3 = load_list(offs3, "idx3")
         idx4 = load_list(offs4, "idx4")
         idx5 = load_list(offs5, "idx5")
         ws_w = load_words(bytes_of(ws_words), N, U32, "ws_w")
         wb_w = load_words(bytes_of(wb_words), N, U32, "wb_w")
-        ws_s = load_plane(ws_scales, nc.vector, nc.sync, "ws_s")
-        wb_s = load_plane(wb_scales, nc.vector, nc.sync, "wb_s")
+        load_rows(ws_s, ws_scales, range(4))
+        load_rows(wb_s, wb_scales, range(4))
 
         boards = [sb.tile([P, C], F32, name="board%d" % t) for t in range(PACK)]
         for board in boards:
             nc.vector.memset(board[:], 0.0)
 
         tok_w = gather(xt_w, idx, U16, "tok_w")
-        note_w = gather(xo_w, idx2, U32, "note_w")
         tok_s = gather(xt_s, idx, U8, "tok_s")
+        note_w = gather(xo_w, idx2, U32, "note_w")
         note_s = gather(xo_s, idx2, U8, "note_s")
-        wd_w = deal_words(w_w, "wd_w")
-        w0d_w = deal_words(w0_w, "w0d_w")
-        wd_s = deal_plane(w_s, "wd_s")
-        w0d_s = deal_plane(w0_s, "w0d_s")
+        wd_w = deal_words(w_w, 1, "wd_w")
+        w0d_w = deal_words(w0_w, 2, "w0d_w")
+        wd_s = deal_plane(w_s, 1, "wd_s")
+        w0d_s = deal_plane(w0_s, 2, "w0d_s")
 
         banks = [ps.tile([P, J], F32, name="a_bank%d" % t) for t in range(PACK)]
         for t in range(PACK):
@@ -114,33 +128,23 @@ def tile_list_readtwice_bank_further_plain_kernel(
                 rhs=note_w[:].bitcast(E5M2), rhs_scale=note_s[:], start=False, stop=True,
             )
 
-        far_w = gather(xt_w, idx6, U16, "far_w")
-        far_s = gather(xt_s, idx6, U8, "far_s")
-        y_banks = [ps.tile([P, O], F32, name="y_bank%d" % u) for u in range(N // P)]
-        for u in range(N // P):
-            cols = slice(P * u, P * (u + 1))
-            nc.tensor.matmul_mx(
-                out=y_banks[u][:], lhsT=ws_w[:, cols].bitcast(E4M3), lhsT_scale=ws_s[:, cols],
-                rhs=far_w[:].bitcast(E2M1), rhs_scale=far_s[:], start=True, stop=False,
-            )
-
-        first = sb.tile([P, PACK, O], F32, name="first")
-        second = sb.tile([P, PACK, O], F32, name="second")
+        first = [sb.tile([P, 2, O], F32, name="first%d" % h) for h in range(2)]
+        second = [sb.tile([P, 2, O], F32, name="second%d" % h) for h in range(2)]
         hid = sb.tile([P, O * PACK], BF16, name="hid", align_bytes=64)
         hid_view = hid[:].rearrange("p (c i t) -> p c t i", t=PACK, i=4)
         a = [sb.tile([P, J], F32, name="a%d" % t) for t in range(PACK)]
 
         def look_v(dst, t, offsets):
-            nc.vector.tensor_copy(dst[:, t, :], boards[t][:].indirect(offsets[:]))
+            nc.vector.tensor_copy(dst[t // 2][:, t % 2, :], boards[t][:].indirect(offsets[:]))
 
         def look_s(dst, t, offsets):
-            nc.scalar.activation(dst[:, t, :], boards[t][:].indirect(offsets[:]), COPY)
+            nc.scalar.activation(dst[t // 2][:, t % 2, :], boards[t][:].indirect(offsets[:]), COPY)
 
-        def larger(rows):
+        def larger(h):
             nc.vector.tensor_tensor(
-                hid_view[:, :, rows, :],
-                first[:, rows, :].rearrange("p t (c i) -> p c t i", i=4),
-                second[:, rows, :].rearrange("p t (c i) -> p c t i", i=4),
+                hid_view[:, :, 2 * h : 2 * h + 2, :],
+                first[h][:].rearrange("p t (c i) -> p c t i", i=4),
+                second[h][:].rearrange("p t (c i) -> p c t i", i=4),
                 MAX,
             )
 
@@ -153,15 +157,25 @@ def tile_list_readtwice_bank_further_plain_kernel(
         nc.scalar.copy(a[3][:], banks[3][:])
         look_s(second, 1, idx5)
         nc.scalar.activation(boards[3][:].indirect(idx3[:]), a[3][:], COPY)
+        far_w = gather(xt_w, idx6, U16, "far_w")
+        far_s = gather(xt_s, idx6, U8, "far_s")
+        y_banks = [ps.tile([P, O], F32, name="y_bank%d" % u) for u in range(N // P)]
+        for u in range(N // P):
+            cols = slice(P * u, P * (u + 1))
+            nc.tensor.matmul_mx(
+                out=y_banks[u][:], lhsT=ws_w[:, cols].bitcast(E4M3), lhsT_scale=ws_s[:, cols],
+                rhs=far_w[:].bitcast(E2M1), rhs_scale=far_s[:], start=True, stop=False,
+            )
+
         look_v(first, 0, idx4)
         look_v(second, 0, idx5)
         look_v(first, 1, idx4)
         look_v(first, 2, idx4)
-        larger(slice(0, 2))
         look_v(second, 2, idx5)
+        larger(0)
         look_s(first, 3, idx4)
         look_s(second, 3, idx5)
-        larger(slice(2, 4))
+        larger(1)
 
         hid_w = sb.tile([P, O], U32, name="hid_w", align_bytes=64)
         hid_s = sb.tile([P, O], U8, name="hid_s", align_bytes=64)

@@ -56,25 +56,17 @@ def tile_list_readtwice_bank_further_plain_kernel(
             nc.vector.tensor_copy(tile[:], window[:].indirect(offsets[:]))
             return tile
 
-        def deal_words(words, parts, name):
-            dealt = sb.tile([P, R], U32, name=name, align_bytes=64)
-            for t0 in range(0, PACK, PACK // parts):
-                ts = slice(t0, t0 + PACK // parts)
-                nc.scalar.copy(
-                    dealt[:].rearrange("p (t c i) -> p c t i", t=PACK, i=4)[:, :, ts, :],
-                    words[:].rearrange("p (c i t) -> p c t i", t=PACK, i=4)[:, :, ts, :],
-                )
-            return dealt
+        def deal_words(dealt, words, ts):
+            nc.scalar.copy(
+                dealt[:].rearrange("p (t c i) -> p c t i", t=PACK, i=4)[:, :, ts, :],
+                words[:].rearrange("p (c i t) -> p c t i", t=PACK, i=4)[:, :, ts, :],
+            )
 
-        def deal_plane(plane, parts, name):
-            dealt = sb.tile([P, R], U8, name=name, align_bytes=64)
-            for t0 in range(0, PACK, PACK // parts):
-                ts = slice(t0, t0 + PACK // parts)
-                nc.vector.tensor_copy(
-                    dealt[:].rearrange("p (t m) -> p t m", t=PACK)[:, ts, :],
-                    plane[:].rearrange("p (m t) -> p t m", t=PACK)[:, ts, :],
-                )
-            return dealt
+        def deal_plane(dealt, plane, ts):
+            nc.vector.tensor_copy(
+                dealt[:].rearrange("p (t m) -> p t m", t=PACK)[:, ts, :],
+                plane[:].rearrange("p (m t) -> p t m", t=PACK)[:, ts, :],
+            )
 
         xt_s = plane_for(xt_scales, nc.vector, "xt_s")
         xo_s = plane_for(xo_scales, nc.vector, "xo_s")
@@ -111,22 +103,33 @@ def tile_list_readtwice_bank_further_plain_kernel(
         tok_s = gather(xt_s, idx, U8, "tok_s")
         note_w = gather(xo_w, idx2, U32, "note_w")
         note_s = gather(xo_s, idx2, U8, "note_s")
-        wd_w = deal_words(w_w, 1, "wd_w")
-        w0d_w = deal_words(w0_w, 2, "w0d_w")
-        wd_s = deal_plane(w_s, 1, "wd_s")
-        w0d_s = deal_plane(w0_s, 2, "w0d_s")
+        wd_w = sb.tile([P, R], U32, name="wd_w", align_bytes=64)
+        w0d_w = sb.tile([P, R], U32, name="w0d_w", align_bytes=64)
+        wd_s = sb.tile([P, R], U8, name="wd_s", align_bytes=64)
+        w0d_s = sb.tile([P, R], U8, name="w0d_s", align_bytes=64)
+        deal_words(wd_w, w_w, slice(0, PACK))
+        for ts in (slice(0, 2), slice(2, 4)):
+            deal_words(w0d_w, w0_w, ts)
+            deal_plane(wd_s, w_s, ts)
+            deal_plane(w0d_s, w0_s, ts)
 
-        banks = [ps.tile([P, J], F32, name="a_bank%d" % t) for t in range(PACK)]
-        for t in range(PACK):
-            cols = slice(P * t, P * (t + 1))
-            nc.tensor.matmul_mx(
-                out=banks[t][:], lhsT=wd_w[:, cols].bitcast(E5M2), lhsT_scale=wd_s[:, cols],
-                rhs=tok_w[:].bitcast(E2M1), rhs_scale=tok_s[:], start=True, stop=False,
-            )
-            nc.tensor.matmul_mx(
-                out=banks[t][:], lhsT=w0d_w[:, cols].bitcast(E4M3), lhsT_scale=w0d_s[:, cols],
-                rhs=note_w[:].bitcast(E5M2), rhs_scale=note_s[:], start=False, stop=True,
-            )
+        def hidden(ts):
+            banks = [ps.tile([P, J], F32, name="a_bank%d" % t, tag="a_bank%d" % (t % 2)) for t in ts]
+            for t, bank in zip(ts, banks):
+                cols = slice(P * t, P * (t + 1))
+                nc.tensor.matmul_mx(
+                    out=bank[:], lhsT=wd_w[:, cols].bitcast(E5M2), lhsT_scale=wd_s[:, cols],
+                    rhs=tok_w[:].bitcast(E2M1), rhs_scale=tok_s[:], start=True, stop=False,
+                )
+            for t, bank in zip(ts, banks):
+                cols = slice(P * t, P * (t + 1))
+                nc.tensor.matmul_mx(
+                    out=bank[:], lhsT=w0d_w[:, cols].bitcast(E4M3), lhsT_scale=w0d_s[:, cols],
+                    rhs=note_w[:].bitcast(E5M2), rhs_scale=note_s[:], start=False, stop=True,
+                )
+            return banks
+
+        banks = hidden((0, 1))
 
         first = [sb.tile([P, 2, O], F32, name="first%d" % h) for h in range(2)]
         second = [sb.tile([P, 2, O], F32, name="second%d" % h) for h in range(2)]
@@ -148,15 +151,6 @@ def tile_list_readtwice_bank_further_plain_kernel(
                 MAX,
             )
 
-        nc.vector.tensor_copy(a[0][:], banks[0][:])
-        nc.scalar.copy(a[1][:], banks[1][:])
-        nc.scalar.copy(a[2][:], banks[2][:])
-        nc.vector.tensor_copy(boards[0][:].indirect(idx3[:]), a[0][:])
-        nc.scalar.activation(boards[1][:].indirect(idx3[:]), a[1][:], COPY)
-        nc.vector.tensor_copy(boards[2][:].indirect(idx3[:]), a[2][:])
-        nc.scalar.copy(a[3][:], banks[3][:])
-        look_s(second, 1, idx5)
-        nc.scalar.activation(boards[3][:].indirect(idx3[:]), a[3][:], COPY)
         far_w = gather(xt_w, idx6, U16, "far_w")
         far_s = gather(xt_s, idx6, U8, "far_s")
         y_banks = [ps.tile([P, O], F32, name="y_bank%d" % u) for u in range(N // P)]
@@ -167,13 +161,23 @@ def tile_list_readtwice_bank_further_plain_kernel(
                 rhs=far_w[:].bitcast(E2M1), rhs_scale=far_s[:], start=True, stop=False,
             )
 
-        look_v(first, 0, idx4)
-        look_v(second, 0, idx5)
+        nc.scalar.copy(a[0][:], banks[0][:])
+        nc.vector.tensor_copy(a[1][:], banks[1][:])
+        banks = hidden((2, 3))
+        nc.scalar.activation(boards[0][:].indirect(idx3[:]), a[0][:], COPY)
+        nc.vector.tensor_copy(boards[1][:].indirect(idx3[:]), a[1][:])
+        nc.scalar.copy(a[2][:], banks[0][:])
+        nc.vector.tensor_copy(a[3][:], banks[1][:])
+        look_s(first, 0, idx4)
         look_v(first, 1, idx4)
-        look_v(first, 2, idx4)
-        look_v(second, 2, idx5)
+        look_v(second, 1, idx5)
+        nc.scalar.activation(boards[2][:].indirect(idx3[:]), a[2][:], COPY)
+        nc.vector.tensor_copy(boards[3][:].indirect(idx3[:]), a[3][:])
+        look_s(second, 0, idx5)
+        look_s(first, 2, idx4)
+        look_s(second, 2, idx5)
         larger(0)
-        look_s(first, 3, idx4)
+        look_v(first, 3, idx4)
         look_s(second, 3, idx5)
         larger(1)
 

@@ -34,9 +34,9 @@ def tile_list_readtwice_bank_further_plain_kernel(
             nc.sync.dma_start(tile[:], src)
             return tile
 
-        def load_words(src, width, dtype, name):
+        def load_words(queue, src, width, dtype, name):
             tile = sb.tile([P, width], dtype, name=name, align_bytes=64)
-            nc.sync.dma_start(tile[:].bitcast(I32), src.bitcast(I32))
+            queue.dma_start(tile[:].bitcast(I32), src.bitcast(I32))
             return tile
 
         def plane_for(src, clear, name):
@@ -75,23 +75,22 @@ def tile_list_readtwice_bank_further_plain_kernel(
         ws_s = plane_for(ws_scales, nc.vector, "ws_s")
         wb_s = plane_for(wb_scales, nc.vector, "wb_s")
 
+        w_w = load_words(nc.gpsimd, bytes_of(w_words), R, U32, "w_w")
+        w0_w = load_words(nc.gpsimd, bytes_of(w0_words), R, U32, "w0_w")
         idx = load_list(offs, "idx")
         idx2 = load_list(offs2, "idx2")
-        xt_w = load_words(xt_words[0], T, U16, "xt_w")
+        xt_w = load_words(nc.sync, xt_words[0], T, U16, "xt_w")
         load_rows(xt_s, xt_scales, range(4))
-        xo_w = load_words(bytes_of(xo_words), Z, U32, "xo_w")
+        xo_w = load_words(nc.sync, bytes_of(xo_words), Z, U32, "xo_w")
         load_rows(xo_s, xo_scales, range(4))
-        load_rows(w_s, w_scales, range(2))
-        w_w = load_words(bytes_of(w_words), R, U32, "w_w")
-        w0_w = load_words(bytes_of(w0_words), R, U32, "w0_w")
-        load_rows(w_s, w_scales, range(2, 4))
+        load_rows(w_s, w_scales, range(4))
         load_rows(w0_s, w0_scales, range(4))
         idx6 = load_list(offs6, "idx6")
         idx3 = load_list(offs3, "idx3")
         idx4 = load_list(offs4, "idx4")
         idx5 = load_list(offs5, "idx5")
-        ws_w = load_words(bytes_of(ws_words), N, U32, "ws_w")
-        wb_w = load_words(bytes_of(wb_words), N, U32, "wb_w")
+        ws_w = load_words(nc.sync, bytes_of(ws_words), N, U32, "ws_w")
+        wb_w = load_words(nc.sync, bytes_of(wb_words), N, U32, "wb_w")
         load_rows(ws_s, ws_scales, range(4))
         load_rows(wb_s, wb_scales, range(4))
 

@@ -75,13 +75,16 @@ def tile_list_readtwice_bank_further_plain_kernel(
         ws_s = plane_for(ws_scales, nc.vector, "ws_s")
         wb_s = plane_for(wb_scales, nc.vector, "wb_s")
 
+        xo_w = sb.tile([P, Z], U32, name="xo_w", align_bytes=64)
+        xo_src = bytes_of(xo_words).bitcast(I32)
+        nc.gpsimd.dma_start(xo_w[:, Z // 2 :].bitcast(I32), xo_src[:, Z // 2 :])
         w_w = load_words(nc.gpsimd, bytes_of(w_words), R, U32, "w_w")
         w0_w = load_words(nc.gpsimd, bytes_of(w0_words), R, U32, "w0_w")
         idx = load_list(offs, "idx")
         idx2 = load_list(offs2, "idx2")
         xt_w = load_words(nc.sync, xt_words[0], T, U16, "xt_w")
         load_rows(xt_s, xt_scales, range(4))
-        xo_w = load_words(nc.sync, bytes_of(xo_words), Z, U32, "xo_w")
+        nc.sync.dma_start(xo_w[:, : Z // 2].bitcast(I32), xo_src[:, : Z // 2])
         load_rows(xo_s, xo_scales, range(4))
         load_rows(w_s, w_scales, range(4))
         load_rows(w0_s, w0_scales, range(4))

from contextlib import ExitStack

import concourse.mybir as mybir

F32 = mybir.dt.float32
BF16 = mybir.dt.bfloat16
I32 = mybir.dt.int32
U32 = mybir.dt.uint32
U16 = mybir.dt.uint16
U8 = mybir.dt.uint8
E4M3 = mybir.dt.float8_e4m3fn_x4
E5M2 = mybir.dt.float8_e5m2_x4
E2M1 = mybir.dt.float4_e2m1fn_x4
COPY = mybir.ActivationFunctionType.Copy
MAX = mybir.AluOpType.max

P = 128
PACK = 4
T, Z, J, R, C, O, N = 1024, 1024, 256, 512, 512, 128, 256
FLOPS = 2 * 512 * (2 * R * J + 2 * N * O)


def tile_list_readtwice_bank_further_plain_kernel(
    tc, xt_words, xt_scales, w_words, w_scales, xo_words, xo_scales, w0_words, w0_scales,
    wb_words, wb_scales, ws_words, ws_scales, offs, offs2, offs3, offs4, offs5, offs6, out,
):
    nc = tc.nc
    with ExitStack() as ctx:
        sb = ctx.enter_context(tc.tile_pool(name="sb", bufs=1))
        ps = ctx.enter_context(tc.psum_pool(name="ps", bufs=1))

        def load_list(src, name):
            tile = sb.tile(list(src.shape), U16, name=name)
            nc.sync.dma_start(tile[:], src)
            return tile

        def load_words(queue, src, width, dtype, name):
            tile = sb.tile([P, width], dtype, name=name, align_bytes=64)
            queue.dma_start(tile[:].bitcast(I32), src.bitcast(I32))
            return tile

        def plane_for(src, clear, name):
            tile = sb.tile([P, src.shape[2]], U8, name=name, align_bytes=64)
            clear.memset(tile[:].bitcast(I32), 0)
            return tile

        def load_rows(tile, src, quadrants):
            for q in quadrants:
                nc.sync.dma_start(tile[32 * q : 32 * q + 4, :].bitcast(I32), src[0, 4 * q : 4 * q + 4, :].bitcast(I32))

        def bytes_of(words):
            return words[0].rearrange("p n t -> p (n t)")

        def gather(window, offsets, dtype, name):
            tile = sb.tile([P, 16 * offsets.shape[1]], dtype, name=name, align_bytes=64)
            nc.vector.tensor_copy(tile[:], window[:].indirect(offsets[:]))
            return tile

        def deal_words(dealt, words, ts):
            nc.scalar.copy(
                dealt[:].rearrange("p (t c i) -> p c t i", t=PACK, i=4)[:, :, ts, :],
                words[:].rearrange("p (c i t) -> p c t i", t=PACK, i=4)[:, :, ts, :],
            )

        def deal_plane(dealt, plane, ts):
            nc.vector.tensor_copy(
                dealt[:].rearrange("p (t m) -> p t m", t=PACK)[:, ts, :],
                plane[:].rearrange("p (m t) -> p t m", t=PACK)[:, ts, :],
            )

        xt_s = plane_for(xt_scales, nc.vector, "xt_s")
        xo_s = plane_for(xo_scales, nc.vector, "xo_s")
        w_s = plane_for(w_scales, nc.vector, "w_s")
        w0_s = plane_for(w0_scales, nc.vector, "w0_s")
        ws_s = plane_for(ws_scales, nc.vector, "ws_s")
        wb_s = plane_for(wb_scales, nc.vector, "wb_s")

        xo_w = sb.tile([P, Z], U32, name="xo_w", align_bytes=64)
        xo_src = bytes_of(xo_words).bitcast(I32)
        nc.gpsimd.dma_start(xo_w[:, Z // 2 :].bitcast(I32), xo_src[:, Z // 2 :])
        w_w = load_words(nc.gpsimd, bytes_of(w_words), R, U32, "w_w")
        w0_w = load_words(nc.gpsimd, bytes_of(w0_words), R, U32, "w0_w")
        idx = load_list(offs, "idx")
        idx2 = load_list(offs2, "idx2")
        xt_w = load_words(nc.sync, xt_words[0], T, U16, "xt_w")
        load_rows(xt_s, xt_scales, range(4))
        nc.sync.dma_start(xo_w[:, : Z // 2].bitcast(I32), xo_src[:, : Z // 2])
        load_rows(xo_s, xo_scales, range(4))
        load_rows(w_s, w_scales, range(4))
        load_rows(w0_s, w0_scales, range(4))
        idx6 = load_list(offs6, "idx6")
        idx3 = load_list(offs3, "idx3")
        idx4 = load_list(offs4, "idx4")
        idx5 = load_list(offs5, "idx5")
        ws_w = load_words(nc.sync, bytes_of(ws_words), N, U32, "ws_w")
        wb_w = load_words(nc.sync, bytes_of(wb_words), N, U32, "wb_w")
        load_rows(ws_s, ws_scales, range(4))
        load_rows(wb_s, wb_scales, range(4))

        boards = [sb.tile([P, C], F32, name="board%d" % t) for t in range(PACK)]
        for board in boards:
            nc.vector.memset(board[:], 0.0)

        tok_w = gather(xt_w, idx, U16, "tok_w")
        tok_s = gather(xt_s, idx, U8, "tok_s")
        note_w = gather(xo_w, idx2, U32, "note_w")
        note_s = gather(xo_s, idx2, U8, "note_s")
        wd_w = sb.tile([P, R], U32, name="wd_w", align_bytes=64)
        w0d_w = sb.tile([P, R], U32, name="w0d_w", align_bytes=64)
        wd_s = sb.tile([P, R], U8, name="wd_s", align_bytes=64)
        w0d_s = sb.tile([P, R], U8, name="w0d_s", align_bytes=64)
        deal_words(wd_w, w_w, slice(0, PACK))
        for ts in (slice(0, 2), slice(2, 4)):
            deal_words(w0d_w, w0_w, ts)
            deal_plane(wd_s, w_s, ts)
            deal_plane(w0d_s, w0_s, ts)

        def hidden(ts):
            banks = [ps.tile([P, J], F32, name="a_bank%d" % t, tag="a_bank%d" % (t % 2)) for t in ts]
            for t, bank in zip(ts, banks):
                cols = slice(P * t, P * (t + 1))
                nc.tensor.matmul_mx(
                    out=bank[:], lhsT=wd_w[:, cols].bitcast(E5M2), lhsT_scale=wd_s[:, cols],
                    rhs=tok_w[:].bitcast(E2M1), rhs_scale=tok_s[:], start=True, stop=False,
                )
            for t, bank in zip(ts, banks):
                cols = slice(P * t, P * (t + 1))
                nc.tensor.matmul_mx(
                    out=bank[:], lhsT=w0d_w[:, cols].bitcast(E4M3), lhsT_scale=w0d_s[:, cols],
                    rhs=note_w[:].bitcast(E5M2), rhs_scale=note_s[:], start=False, stop=True,
                )
            return banks

        banks = hidden((0, 1))

        first = [sb.tile([P, 2, O], F32, name="first%d" % h) for h in range(2)]
        second = [sb.tile([P, 2, O], F32, name="second%d" % h) for h in range(2)]
        hid = sb.tile([P, O * PACK], BF16, name="hid", align_bytes=64)
        hid_view = hid[:].rearrange("p (c i t) -> p c t i", t=PACK, i=4)
        a = [sb.tile([P, J], F32, name="a%d" % t) for t in range(PACK)]

        def look_v(dst, t, offsets):
            nc.vector.tensor_copy(dst[t // 2][:, t % 2, :], boards[t][:].indirect(offsets[:]))

        def look_s(dst, t, offsets):
            nc.scalar.activation(dst[t // 2][:, t % 2, :], boards[t][:].indirect(offsets[:]), COPY)

        def larger(h):
            nc.vector.tensor_tensor(
                hid_view[:, :, 2 * h : 2 * h + 2, :],
                first[h][:].rearrange("p t (c i) -> p c t i", i=4),
                second[h][:].rearrange("p t (c i) -> p c t i", i=4),
                MAX,
            )

        far_w = gather(xt_w, idx6, U16, "far_w")
        far_s = gather(xt_s, idx6, U8, "far_s")
        y_banks = [ps.tile([P, O], F32, name="y_bank%d" % u) for u in range(N // P)]
        for u in range(N // P):
            cols = slice(P * u, P * (u + 1))
            nc.tensor.matmul_mx(
                out=y_banks[u][:], lhsT=ws_w[:, cols].bitcast(E4M3), lhsT_scale=ws_s[:, cols],
                rhs=far_w[:].bitcast(E2M1), rhs_scale=far_s[:], start=True, stop=False,
            )

        nc.scalar.copy(a[0][:], banks[0][:])
        nc.vector.tensor_copy(a[1][:], banks[1][:])
        banks = hidden((2, 3))
        nc.scalar.activation(boards[0][:].indirect(idx3[:]), a[0][:], COPY)
        nc.vector.tensor_copy(boards[1][:].indirect(idx3[:]), a[1][:])
        nc.scalar.copy(a[2][:], banks[0][:])
        nc.vector.tensor_copy(a[3][:], banks[1][:])
        look_s(first, 0, idx4)
        look_v(first, 1, idx4)
        look_v(second, 1, idx5)
        nc.scalar.activation(boards[2][:].indirect(idx3[:]), a[2][:], COPY)
        nc.vector.tensor_copy(boards[3][:].indirect(idx3[:]), a[3][:])
        look_s(second, 0, idx5)
        look_s(first, 2, idx4)
        look_s(second, 2, idx5)
        larger(0)
        look_v(first, 3, idx4)
        look_s(second, 3, idx5)
        larger(1)

        hid_w = sb.tile([P, O], U32, name="hid_w", align_bytes=64)
        hid_s = sb.tile([P, O], U8, name="hid_s", align_bytes=64)
        nc.vector.quantize_mx(out=hid_w[:].bitcast(E5M2), scales=hid_s[:], in_=hid[:])

        for u in range(N // P):
            cols = slice(P * u, P * (u + 1))
            nc.tensor.matmul_mx(
                out=y_banks[u][:], lhsT=wb_w[:, cols].bitcast(E4M3), lhsT_scale=wb_s[:, cols],
                rhs=hid_w[:].bitcast(E5M2), rhs_scale=hid_s[:], start=False, stop=True,
            )
        y0 = sb.tile([P, O], F32, name="y0")
        nc.vector.tensor_copy(y0[:], y_banks[0][:])
        nc.sync.dma_start(out[0:P, :], y0[:])
        y1 = sb.tile([P, O], F32, name="y1")
        nc.scalar.copy(y1[:], y_banks[1][:])
        nc.scalar.dma_start(out[P : 2 * P, :], y1[:])
